import numpy as np
import ml_dtypes


def mxq(x, axis, fmt="e4m3"):
    dtype, down = {"e4m3": (ml_dtypes.float8_e4m3fn, 7), "e5m2": (ml_dtypes.float8_e5m2, 14)}[fmt]
    v = np.moveaxis(np.asarray(x, np.float32).astype(ml_dtypes.bfloat16).astype(np.float64), axis, -1)
    blocks = v.reshape(v.shape[:-1] + (-1, 32))
    amax = np.abs(blocks).max(-1, keepdims=True)
    byte = np.maximum(np.where(amax > 0, np.frexp(amax)[1] - 1 + 127, 0) - down, 1)
    scale = np.exp2(byte - 127.0)
    codes = (blocks / scale).astype(np.float32).astype(dtype).astype(np.float64)
    return np.moveaxis((codes * scale).reshape(v.shape), -1, axis)


WIDE = False


def mx_kscale(k):
    if not WIDE:
        return np.ones(k)
    levels = np.array([10, -10, 5, -5, 0])
    if k % 512:
        return np.exp2(np.random.permutation(np.resize(levels, k // 32))).repeat(32)
    a = np.empty((k // 512, 16))
    for p in range(k // 512):
        a[p, :8] = np.random.permutation(np.resize(levels, 8))
        for g in range(8):
            far = levels[np.abs(levels - a[p, g]) >= 10]
            a[p, g + 8] = far[np.random.randint(len(far))]
    return np.exp2(a.ravel()).repeat(32)


BF16 = ml_dtypes.bfloat16


def bf(x):
    return np.asarray(x, np.float32).astype(BF16)


def f64(x):
    return np.asarray(x).astype(np.float64)


E2M1 = np.array([0.0, 0.5, 1.0, 1.5, 2.0, 3.0, 4.0, 6.0, -0.0, -0.5, -1.0, -1.5, -2.0, -3.0, -4.0, -6.0])


def pack_weight(w, fmt):
    k, n = w.shape
    w = f64(bf(w)).reshape(k // 32, 32, n)
    amax = np.abs(w).max(1)
    if fmt == "e4m3":
        byte = np.frexp(amax)[1] - 1 + 127 - 7
    else:
        mant, ex = np.frexp(amax / 6.0)
        byte = np.where(mant > 0.5, ex, ex - 1) + 127
    byte = np.clip(np.where(amax > 0, byte, 1), 1, 254)
    scaled = (w * np.exp2(127.0 - byte)[:, None, :]).reshape(k, n).astype(np.float32)
    by_word = np.ascontiguousarray(scaled.reshape(k // 512, 128, 4, n).transpose(0, 1, 3, 2))
    if fmt == "e4m3":
        words = by_word.astype(ml_dtypes.float8_e4m3fn).view(np.uint8)
    else:
        c = by_word.astype(ml_dtypes.float4_e2m1fn).view(np.uint8) & 0xF
        words = c[..., 0::2] | (c[..., 1::2] << 4)
    return np.ascontiguousarray(words), np.ascontiguousarray(byte.astype(np.uint8).reshape(k // 512, 16, n))


def unpack_weight(words, scales, fmt):
    g, p, n, _ = words.shape
    if fmt == "e4m3":
        vals = np.ascontiguousarray(words).view(ml_dtypes.float8_e4m3fn).astype(np.float64)
    else:
        nib = np.empty((g, p, n, 4), np.uint8)
        nib[..., 0::2] = words & 0xF
        nib[..., 1::2] = words >> 4
        vals = E2M1[nib]
    vals = vals * np.repeat(np.exp2(scales.astype(np.float64) - 127.0), 8, axis=1)[..., None]
    return vals.transpose(0, 1, 3, 2).reshape(g * 512, n)
def pack4(w):
    words, scales = pack_weight(w, "e2m1")
    return words.reshape(words.shape[0], 128, -1), scales


def unpack4(words, scales):
    return unpack_weight(words.reshape(words.shape[0], 128, -1, 2), scales, "e2m1")


def planes(Y):
    n, m = Y.shape
    b = f64(bf(Y)).reshape(n // 32, 32, m)
    amax = np.abs(b).max(1)
    byte = np.clip(np.where(amax > 0, np.frexp(amax)[1] - 1 + 127 - 7, 1), 1, 254)
    codes = (b * np.exp2(127.0 - byte)[:, None, :]).reshape(n, m).astype(np.float32).astype(ml_dtypes.float8_e4m3fn).view(np.uint8)
    words = codes.reshape(n // 512, 128, 4, m).transpose(0, 1, 3, 2)
    return np.ascontiguousarray(words), np.ascontiguousarray(byte.astype(np.uint8).reshape(n // 512, 16, m))


S, RU, RT, Q = 1024, 1024, 512, 1536


def setup_inputs():
    s = mx_kscale(RU)
    t = mx_kscale(RT)
    a = bf(np.random.randn(S, RU) / s)
    c = bf(np.random.randn(S, RT) / t)
    ux_words, ux_scales = pack4(np.random.randn(RU, Q) / np.sqrt(RU) * s[:, None])
    uy_words, uy_scales = pack4(np.random.randn(RU, Q) / np.sqrt(RU) * s[:, None])
    tx_words, tx_scales = pack4(np.random.randn(RT, Q) / np.sqrt(RT) * t[:, None])
    ty_words, ty_scales = pack4(np.random.randn(RT, Q) / np.sqrt(RT) * t[:, None])
    w = bf(np.exp(0.8 * np.random.randn(Q)))
    return {"a": a, "c": c, "ux_words": ux_words, "ux_scales": ux_scales,
            "uy_words": uy_words, "uy_scales": uy_scales,
            "tx_words": tx_words, "tx_scales": tx_scales,
            "ty_words": ty_words, "ty_scales": ty_scales, "w": w}

def reference(a, c, ux_words, ux_scales, uy_words, uy_scales, tx_words, tx_scales, ty_words, ty_scales, w):
    aq = mxq(f64(a), 1, "e4m3")
    cq = mxq(f64(c), 1, "e4m3")
    vx = aq @ unpack4(ux_words, ux_scales)
    vy = aq @ unpack4(uy_words, uy_scales)
    dx = cq @ unpack4(tx_words, tx_scales)
    dy = cq @ unpack4(ty_words, ty_scales)
    y = f64(w) * (vx * dx + vy * dy)
    Y = y.T
    words, scales = planes(Y)
    return y, words, scales

@@ -1,0 +1,312 @@
+from contextlib import ExitStack
+
+import concourse.mybir as mybir
+from concourse.masks import make_identity
+
+S, RU, RT, Q = 1024, 1024, 512, 1536
+FLOPS = 2 * S * Q * (2 * RU + 2 * RT)
+
+F32 = mybir.dt.float32
+BF16 = mybir.dt.bfloat16
+U32 = mybir.dt.uint32
+I32 = mybir.dt.int32
+U8 = mybir.dt.uint8
+FP8X4 = mybir.dt.float8_e4m3fn_x4
+FP4X4 = mybir.dt.float4_e2m1fn_x4
+MULT = mybir.AluOpType.mult
+ADD = mybir.AluOpType.add
+
+P = 128
+N = 512
+TILES = S // P
+CHUNKS = Q // N
+STEPS = TILES * CHUNKS
+
+
+def tile_reduced_heat_convection_g4_kernel(
+    tc, a, c, ux_words, ux_scales, uy_words, uy_scales, tx_words, tx_scales, ty_words, ty_scales, w,
+    out_0, out_1, out_2,
+):
+    nc = tc.nc
+    with ExitStack() as ctx:
+        keep = ctx.enter_context(tc.tile_pool(name="keep", bufs=1))
+        work = ctx.enter_context(tc.tile_pool(name="work", bufs=3))
+        psum = ctx.enter_context(tc.psum_pool(name="psum", bufs=1))
+        ctx.enter_context(tc.manual_schedule())
+
+        words_in = {"tx": tx_words, "ty": ty_words, "ux": ux_words, "uy": uy_words}
+        scales_in = {"tx": tx_scales, "ty": ty_scales, "ux": ux_scales, "uy": uy_scales}
+        passes = {"tx": RT // N, "ty": RT // N, "ux": RU // N, "uy": RU // N}
+
+        ident = keep.tile([P, P], F32, name="ident")
+        make_identity(nc, ident[:])
+
+        planes = {}
+        plane_tiles = {}
+
+        def clear_plane(m, first, count):
+            t = keep.tile([P, passes[m], N * count], U8, name="plane_%s_%d" % (m, first), align_bytes=64)
+            nc.vector.memset(t[:].bitcast(I32), 0)
+            plane_tiles[m, first] = t
+            for j in range(count):
+                for g in range(passes[m]):
+                    planes[m, first + j, g] = t[:, g, N * j : N * (j + 1)]
+
+        def load_scales(m, first, count, queue):
+            rows = scales_in[m].bitcast(I32)[:, :, first * N // 4 : (first + count) * N // 4]
+            for quad in range(4):
+                queue.dma_start(
+                    out=plane_tiles[m, first][32 * quad : 32 * quad + 4, :, :].bitcast(I32),
+                    in_=rows[:, 4 * quad : 4 * quad + 4, :].rearrange("g r n -> r g n"),
+                )
+
+        weights = {}
+
+        def load_words(m, first, count):
+            t = keep.tile([P, passes[m], 2 * N * count], U8, name="words_%s_%d" % (m, first), align_bytes=64)
+            src = words_in[m].bitcast(I32)[:, :, first * N // 2 : (first + count) * N // 2]
+            nc.sync.dma_start(out=t[:].bitcast(I32), in_=src.rearrange("g p n -> p g n"))
+            for j in range(count):
+                for g in range(passes[m]):
+                    weights[m, first + j, g] = t[:, g, 2 * N * j : 2 * N * (j + 1)]
+
+        a_rows = {}
+        c_rows = {}
+
+        def load_a(i):
+            a_rows[i] = keep.tile([P, RU], BF16, name="a_rows_%d" % i)
+            nc.sync.dma_start(out=a_rows[i][:], in_=a[i * P : (i + 1) * P, :])
+
+        def load_c(j):
+            c_rows[j] = keep.tile([P, 2, RT], BF16, name="c_rows_%d" % j)
+            nc.sync.dma_start(
+                out=c_rows[j][:], in_=c[2 * j * P : 2 * (j + 1) * P, :].rearrange("(i p) k -> p i k", i=2)
+            )
+
+        w_cols = keep.tile([P, CHUNKS, 4], BF16, name="w_cols")
+        w_cols32 = keep.tile([P, CHUNKS * 4], F32, name="w_cols32")
+
+        for m in ("tx", "ty", "ux", "uy"):
+            clear_plane(m, 0, 1)
+        load_c(0)
+        load_a(0)
+        load_scales("ty", 0, 1, nc.gpsimd)
+        load_scales("tx", 0, 1, nc.sync)
+        load_words("tx", 0, 1)
+        load_words("ux", 0, 1)
+        load_scales("ux", 0, 1, nc.sync)
+        load_words("ty", 0, 1)
+        load_words("uy", 0, 1)
+        load_a(1)
+        load_scales("uy", 0, 1, nc.sync)
+        load_c(1)
+        load_a(2)
+        nc.sync.dma_start(out=w_cols[:], in_=w.rearrange("(g p j) -> p g j", g=CHUNKS, j=4))
+        for m in ("tx", "ty", "ux", "uy"):
+            clear_plane(m, 1, CHUNKS - 1)
+        load_c(2)
+        for i in range(3, TILES):
+            load_a(i)
+            if i == 4:
+                load_c(3)
+        for m in ("tx", "ty", "ux", "uy"):
+            load_scales(m, 1, CHUNKS - 1, nc.sync)
+        for m in ("tx", "ty", "ux", "uy"):
+            load_words(m, 1, CHUNKS - 1)
+
+        out_words = out_1.rearrange("g p m t -> g p (m t)").bitcast(I32)
+        out_scales = out_2.bitcast(I32)
+
+        lhs = {}
+        y_codes = {}
+        y_scales = {}
+        banks = {}
+        grouped = {}
+        d_sb = {}
+        prods = {}
+        sums = {}
+        ys = {}
+        y16 = {}
+        w_bank = {}
+        stored = {}
+
+        def turn(job):
+            bank = psum.tile([P, 2, 2, P], F32, name="turn_bank", bufs=2)
+            banks[job] = bank
+            for h, (kind, i, k) in enumerate(job):
+                for u in range(2):
+                    if kind == "a":
+                        src = a_rows[i][:].bitcast(F32)[:, 256 * k + u : 256 * (k + 1) : 2]
+                    elif kind == "c":
+                        src = c_rows[i // 2][:, i % 2, :].bitcast(F32)[:, u:256:2]
+                    else:
+                        src = y16[i][:].bitcast(F32)[:, P * u : P * (u + 1)]
+                    nc.tensor.transpose(bank[:, h, u, :], src, ident[:])
+
+        def copy_out(job):
+            t = work.tile([P, 2, N], BF16, name="grouped", align_bytes=64)
+            grouped[job] = t[:, : len(job), :].rearrange("p h x -> p (h x)")
+            nc.scalar.copy(
+                out=grouped[job].bitcast(F32).rearrange("p (h s u) -> p h s u", s=P, u=2),
+                in_=banks[job][:, : len(job), :, :].rearrange("p h u s -> p h s u"),
+            )
+
+        def quantize(job):
+            width = P * len(job)
+            if job[0][0] == "y":
+                g, i = divmod(job[0][1], TILES)
+                if i == 0:
+                    y_codes[g] = keep.tile([P, S], U32, name="y_codes_%d" % g, align_bytes=64)
+                    y_scales[g] = keep.tile([P, S], U8, name="y_scales_%d" % g, align_bytes=64)
+                cols = slice(P * i, P * i + width)
+                nc.vector.quantize_mx(
+                    out=y_codes[g][:, cols].bitcast(FP8X4), scales=y_scales[g][:, cols], in_=grouped[job]
+                )
+                done = P * i + width
+                if done % (S // 2) == 0 or job[0][1] >= STEPS - 4:
+                    part = slice(stored.get(g, 0), done)
+                    stored[g] = done
+                    nc.sync.dma_start(out=out_words[g, :, part], in_=y_codes[g][:, part].bitcast(I32))
+                if done == S:
+                    for quad in range(4):
+                        nc.sync.dma_start(
+                            out=out_scales[g, 4 * quad : 4 * quad + 4, :],
+                            in_=y_scales[g][32 * quad : 32 * quad + 4, :].bitcast(I32),
+                        )
+                return
+            codes = keep.tile([P, width], U32, name="codes_%s_%d" % job[0][:2], align_bytes=64)
+            scales = keep.tile([P, width], U8, name="scales_%s_%d" % job[0][:2], align_bytes=64)
+            nc.vector.quantize_mx(out=codes[:].bitcast(FP8X4), scales=scales[:], in_=grouped[job])
+            for h, key in enumerate(job):
+                cols = slice(P * h, P * (h + 1))
+                lhs[key] = (codes[:, cols], scales[:, cols])
+
+        def product(m, n, bank):
+            g, i = divmod(n, TILES)
+            side = "a" if m[0] == "u" else "c"
+            for k in range(passes[m]):
+                codes, scales = lhs[side, i, k]
+                nc.tensor.matmul_mx(
+                    out=bank[:],
+                    lhsT=codes.bitcast(FP8X4),
+                    lhsT_scale=scales,
+                    rhs=weights[m, g, k].bitcast(FP4X4),
+                    rhs_scale=planes[m, g, k],
+                    start=(k == 0),
+                    stop=(k == passes[m] - 1),
+                )
+
+        def gradient(m, n):
+            bank = psum.tile([P, N], F32, name="d_bank", bufs=2)
+            product(m, n, bank)
+            d_sb[m, n] = work.tile([P, N], F32, name="d_" + m)
+            nc.scalar.copy(out=d_sb[m, n][:], in_=bank[:])
+
+        def velocity(m, n):
+            bank = psum.tile([P, N], F32, name="v_bank", bufs=3)
+            product(m, n, bank)
+            return bank
+
+        def multiply(m, n, bank):
+            prods[m, n] = work.tile([P, N], F32, name="prod_" + m)
+            nc.vector.tensor_tensor(out=prods[m, n][:], in0=bank[:], in1=d_sb["t" + m[1], n][:], op=MULT)
+
+        def add(n):
+            sums[n] = work.tile([P, N], F32, name="sum")
+            eng = nc.vector if n == STEPS - 1 else nc.gpsimd
+            eng.tensor_tensor(out=sums[n][:], in0=prods["ux", n][:], in1=prods["uy", n][:], op=ADD)
+
+        def weigh(n):
+            g, i = divmod(n, TILES)
+            ys[n] = work.tile([P, N], F32, name="y", bufs=6)
+            nc.vector.tensor_tensor(
+                out=ys[n][:].rearrange("s (p j) -> s p j", j=4),
+                in0=sums[n][:].rearrange("s (p j) -> s p j", j=4),
+                in1=w_bank[g][:].rearrange("s (j p) -> s p j", j=4),
+                op=MULT,
+            )
+            nc.sync.dma_start(out=out_0[i * P : (i + 1) * P, g * N : (g + 1) * N], in_=ys[n][:])
+
+        def round_y(n):
+            y16[n] = work.tile([P, N], BF16, name="y16", bufs=8)
+            dst = y16[n][:].rearrange("s (u p e) -> s u p e", u=2, e=2)
+            src = ys[n][:].rearrange("s (p u e) -> s u p e", u=2, e=2)
+            if False:
+                nc.gpsimd.tensor_scalar(out=dst, in0=src, scalar1=1.0, scalar2=1.0, op0=MULT, op1=MULT)
+            else:
+                nc.scalar.copy(out=dst, in_=src)
+
+        def spread_w(g):
+            w_bank[g] = psum.tile([P, N], F32, name="w_bank")
+            for j in range(4):
+                col = w_cols32[:, 4 * g + j : 4 * g + j + 1]
+                nc.tensor.transpose(w_bank[g][:, P * j : P * (j + 1)], col.to_broadcast([P, P]), ident[:])
+
+        def a_job(i):
+            return (("a", i, 0), ("a", i, 1))
+
+        def c_job(j):
+            return (("c", 2 * j, 0), ("c", 2 * j + 1, 0))
+
+        def y_job(m):
+            return (("y", 2 * m, 0), ("y", 2 * m + 1, 0))
+
+        runs = {-1: [a_job(1), c_job(1)], 0: [a_job(2), c_job(2)], 1: [a_job(3), a_job(4)], 2: [c_job(3), a_job(5)], 3: [a_job(6), a_job(7)]}
+        for n in range(5, STEPS, 4):
+            runs[n] = [y_job(m) for m in ((n - 7) // 2, (n - 5) // 2) if m >= 0]
+        runs[23] = [y_job(9)]
+        turn(c_job(0))
+        turn(a_job(0))
+        copy_out(c_job(0))
+        quantize(c_job(0))
+        copy_out(a_job(0))
+        gradient("tx", 0)
+        quantize(a_job(0))
+        gradient("tx", 1)
+        multiply("ux", 0, velocity("ux", 0))
+        gradient("ty", 0)
+        turn(a_job(1))
+        turn(c_job(1))
+        nc.vector.tensor_copy(out=w_cols32[:], in_=w_cols[:].rearrange("p g j -> p (g j)"))
+        late = []
+        for n in range(0, STEPS):
+            turned = runs.get(n - 1, [])
+            now = late + [j for j in turned[:1]] + [j for j in turned[1:] if j[0][0] != "y"]
+            late = [j for j in turned[1:] if j[0][0] == "y"]
+            ahead = n + 1 < STEPS
+            if 0 <= n - 2:
+                weigh(n - 2)
+            for job in now[:1]:
+                copy_out(job)
+            if ahead and n > 0:
+                gradient("tx", n + 1)
+            for job in now[1:]:
+                copy_out(job)
+            if n > 0:
+                multiply("ux", n, velocity("ux", n))
+            if ahead:
+                gradient("ty", n + 1)
+            for job in now[:1]:
+                quantize(job)
+            if 0 <= n - 2:
+                round_y(n - 2)
+            for job in now[1:]:
+                quantize(job)
+            multiply("uy", n, velocity("uy", n))
+            add(n)
+            for job in runs.get(n, []):
+                turn(job)
+            if n % TILES == 1:
+                spread_w(n // TILES)
+        weigh(22)
+        weigh(23)
+        turn(y_job(10))
+        copy_out(y_job(9))
+        round_y(22)
+        quantize(y_job(9))
+        round_y(23)
+        turn(y_job(11))
+        copy_out(y_job(10))
+        quantize(y_job(10))
+        copy_out(y_job(11))
+        quantize(y_job(11))

@@ -102,17 +102,11 @@ def tile_reduced_heat_convection_g4_kernel(
         load_c(1)
         load_a(2)
         nc.sync.dma_start(out=w_cols[:], in_=w.rearrange("(g p j) -> p g j", g=CHUNKS, j=4))
-        for m in ("tx", "ty", "ux", "uy"):
-            clear_plane(m, 1, CHUNKS - 1)
         load_c(2)
         for i in range(3, TILES):
             load_a(i)
             if i == 4:
                 load_c(3)
-        for m in ("tx", "ty", "ux", "uy"):
-            load_scales(m, 1, CHUNKS - 1, nc.sync)
-        for m in ("tx", "ty", "ux", "uy"):
-            load_words(m, 1, CHUNKS - 1)
 
         out_words = out_1.rearrange("g p m t -> g p (m t)").bitcast(I32)
         out_scales = out_2.bitcast(I32)
@@ -144,7 +138,7 @@ def tile_reduced_heat_convection_g4_kernel(
                     nc.tensor.transpose(bank[:, h, u, :], src, ident[:])
 
         def copy_out(job):
-            t = work.tile([P, 2, N], BF16, name="grouped", align_bytes=64)
+            t = work.tile([P, 2, N], BF16, name="grouped", bufs=4, align_bytes=64)
             grouped[job] = t[:, : len(job), :].rearrange("p h x -> p (h x)")
             nc.scalar.copy(
                 out=grouped[job].bitcast(F32).rearrange("p (h s u) -> p h s u", s=P, u=2),
@@ -169,7 +163,7 @@ def tile_reduced_heat_convection_g4_kernel(
                     nc.sync.dma_start(out=out_words[g, :, part], in_=y_codes[g][:, part].bitcast(I32))
                 if done == S:
                     for quad in range(4):
-                        nc.sync.dma_start(
+                        (nc.scalar if g == CHUNKS - 1 and quad % 2 else nc.sync).dma_start(
                             out=out_scales[g, 4 * quad : 4 * quad + 4, :],
                             in_=y_scales[g][32 * quad : 32 * quad + 4, :].bitcast(I32),
                         )
@@ -236,6 +230,15 @@ def tile_reduced_heat_convection_g4_kernel(
             else:
                 nc.scalar.copy(out=dst, in_=src)
 
+        def weigh_round(n):
+            y16[n] = work.tile([P, N], BF16, name="y16", bufs=8)
+            nc.vector.tensor_tensor(
+                out=y16[n][:].rearrange("s (u p e) -> s u p e", u=2, e=2),
+                in0=sums[n][:].rearrange("s (p u e) -> s u p e", u=2, e=2),
+                in1=w_bank[n // TILES][:].rearrange("s (u e p) -> s u p e", u=2, e=2),
+                op=MULT,
+            )
+
         def spread_w(g):
             w_bank[g] = psum.tile([P, N], F32, name="w_bank")
             for j in range(4):
@@ -262,6 +265,11 @@ def tile_reduced_heat_convection_g4_kernel(
         copy_out(a_job(0))
         gradient("tx", 0)
         quantize(a_job(0))
+        for m in ("tx", "ty", "ux", "uy"):
+            clear_plane(m, 1, CHUNKS - 1)
+            load_scales(m, 1, CHUNKS - 1, nc.sync)
+        for m in ("tx", "ty", "ux", "uy"):
+            load_words(m, 1, CHUNKS - 1)
         gradient("tx", 1)
         multiply("ux", 0, velocity("ux", 0))
         gradient("ty", 0)
@@ -287,26 +295,30 @@ def tile_reduced_heat_convection_g4_kernel(
             if ahead:
                 gradient("ty", n + 1)
             for job in now[:1]:
-                quantize(job)
+                if ahead:
+                    quantize(job)
             if 0 <= n - 2:
                 round_y(n - 2)
             for job in now[1:]:
                 quantize(job)
             multiply("uy", n, velocity("uy", n))
-            add(n)
+            if ahead:
+                add(n)
             for job in runs.get(n, []):
                 turn(job)
             if n % TILES == 1:
                 spread_w(n // TILES)
         weigh(22)
-        weigh(23)
         turn(y_job(10))
         copy_out(y_job(9))
         round_y(22)
-        quantize(y_job(9))
-        round_y(23)
-        turn(y_job(11))
+        add(23)
+        weigh_round(23)
+        weigh(23)
         copy_out(y_job(10))
+        turn(y_job(11))
+        quantize(y_job(8))
+        quantize(y_job(9))
         quantize(y_job(10))
         copy_out(y_job(11))
         quantize(y_job(11))

@@ -84,7 +84,7 @@ def tile_reduced_heat_convection_g4_kernel(
             )
 
         w_cols = keep.tile([P, CHUNKS, 4], BF16, name="w_cols")
-        w_cols32 = keep.tile([P, CHUNKS * 4], F32, name="w_cols32")
+        w_psum = psum.tile([P, 2, 2, P], F32, name="w_bank")
 
         for m in ("tx", "ty", "ux", "uy"):
             clear_plane(m, 0, 1)
@@ -123,19 +123,30 @@ def tile_reduced_heat_convection_g4_kernel(
         y16 = {}
         w_bank = {}
         stored = {}
+        sorted_rows = {}
 
         def turn(job):
             bank = psum.tile([P, 2, 2, P], F32, name="turn_bank", bufs=2)
             banks[job] = bank
             for h, (kind, i, k) in enumerate(job):
                 for u in range(2):
-                    if kind == "a":
+                    if job in sorted_rows:
+                        src = sorted_rows[job][:, h, u, :]
+                    elif kind == "a":
                         src = a_rows[i][:].bitcast(F32)[:, 256 * k + u : 256 * (k + 1) : 2]
                     elif kind == "c":
                         src = c_rows[i // 2][:, i % 2, :].bitcast(F32)[:, u:256:2]
                     else:
                         src = y16[i][:].bitcast(F32)[:, P * u : P * (u + 1)]
                     nc.tensor.transpose(bank[:, h, u, :], src, ident[:])
+
+        def presort(job):
+            kind, i, k = job[0]
+            rows = a_rows[i][:] if kind == "a" else c_rows[i // 2][:].rearrange("s h k -> s (h k)")
+            sorted_rows[job] = work.tile([P, 2, 2, P], F32, name="sorted_rows", bufs=5)
+            nc.vector.tensor_copy(
+                out=sorted_rows[job][:], in_=rows.bitcast(F32).rearrange("s (h p u) -> s h u p", h=2, u=2)
+            )
 
         def copy_out(job):
             t = work.tile([P, 2, N], BF16, name="grouped", bufs=4, align_bytes=64)
@@ -214,9 +225,9 @@ def tile_reduced_heat_convection_g4_kernel(
             g, i = divmod(n, TILES)
             ys[n] = work.tile([P, N], F32, name="y", bufs=6)
             nc.vector.tensor_tensor(
-                out=ys[n][:].rearrange("s (p j) -> s p j", j=4),
-                in0=sums[n][:].rearrange("s (p j) -> s p j", j=4),
-                in1=w_bank[g][:].rearrange("s (j p) -> s p j", j=4),
+                out=ys[n][:].rearrange("s (p u e) -> s p u e", u=2, e=2),
+                in0=sums[n][:].rearrange("s (p u e) -> s p u e", u=2, e=2),
+                in1=w_bank[g].rearrange("s u p e -> s p u e"),
                 op=MULT,
             )
             nc.sync.dma_start(out=out_0[i * P : (i + 1) * P, g * N : (g + 1) * N], in_=ys[n][:])
@@ -235,15 +246,15 @@ def tile_reduced_heat_convection_g4_kernel(
             nc.vector.tensor_tensor(
                 out=y16[n][:].rearrange("s (u p e) -> s u p e", u=2, e=2),
                 in0=sums[n][:].rearrange("s (p u e) -> s u p e", u=2, e=2),
-                in1=w_bank[n // TILES][:].rearrange("s (u e p) -> s u p e", u=2, e=2),
+                in1=w_bank[n // TILES],
                 op=MULT,
             )
 
         def spread_w(g):
-            w_bank[g] = psum.tile([P, N], F32, name="w_bank")
-            for j in range(4):
-                col = w_cols32[:, 4 * g + j : 4 * g + j + 1]
-                nc.tensor.transpose(w_bank[g][:, P * j : P * (j + 1)], col.to_broadcast([P, P]), ident[:])
+            for u in range(2):
+                col = w_cols[:, g, :].bitcast(F32)[:, u : u + 1]
+                nc.tensor.transpose(w_psum[:, g % 2, u, :], col.to_broadcast([P, P]), ident[:])
+            w_bank[g] = w_psum[:, g % 2, :, :].bitcast(BF16).rearrange("s u (p e) -> s u p e", e=2)
 
         def a_job(i):
             return (("a", i, 0), ("a", i, 1))
@@ -255,9 +266,8 @@ def tile_reduced_heat_convection_g4_kernel(
             return (("y", 2 * m, 0), ("y", 2 * m + 1, 0))
 
         runs = {-1: [a_job(1), c_job(1)], 0: [a_job(2), c_job(2)], 1: [a_job(3), a_job(4)], 2: [c_job(3), a_job(5)], 3: [a_job(6), a_job(7)]}
-        for n in range(5, STEPS, 4):
-            runs[n] = [y_job(m) for m in ((n - 7) // 2, (n - 5) // 2) if m >= 0]
-        runs[23] = [y_job(9)]
+        for n in range(7, STEPS, 4):
+            runs[n] = [y_job((n - 7) // 2), y_job((n - 5) // 2)]
         turn(c_job(0))
         turn(a_job(0))
         copy_out(c_job(0))
@@ -275,7 +285,6 @@ def tile_reduced_heat_convection_g4_kernel(
         gradient("ty", 0)
         turn(a_job(1))
         turn(c_job(1))
-        nc.vector.tensor_copy(out=w_cols32[:], in_=w_cols[:].rearrange("p g j -> p (g j)"))
         late = []
         for n in range(0, STEPS):
             turned = runs.get(n - 1, [])
@@ -295,28 +304,34 @@ def tile_reduced_heat_convection_g4_kernel(
             if ahead:
                 gradient("ty", n + 1)
             for job in now[:1]:
-                if ahead:
-                    quantize(job)
+                quantize(job)
             if 0 <= n - 2:
                 round_y(n - 2)
             for job in now[1:]:
                 quantize(job)
+            for job in runs.get(n + 1, []):
+                if job[0][0] != "y" and n >= 1:
+                    presort(job)
             multiply("uy", n, velocity("uy", n))
             if ahead:
                 add(n)
             for job in runs.get(n, []):
                 turn(job)
-            if n % TILES == 1:
-                spread_w(n // TILES)
+            if n == 1:
+                spread_w(0)
+                spread_w(1)
+            if n == 11:
+                spread_w(2)
         weigh(22)
+        copy_out(y_job(8))
         turn(y_job(10))
         copy_out(y_job(9))
         round_y(22)
         add(23)
         weigh_round(23)
         weigh(23)
-        copy_out(y_job(10))
         turn(y_job(11))
+        copy_out(y_job(10))
         quantize(y_job(8))
         quantize(y_job(9))
         quantize(y_job(10))

from contextlib import ExitStack

import concourse.mybir as mybir
from concourse.masks import make_identity

S, RU, RT, Q = 1024, 1024, 512, 1536
FLOPS = 2 * S * Q * (2 * RU + 2 * RT)

F32 = mybir.dt.float32
BF16 = mybir.dt.bfloat16
U32 = mybir.dt.uint32
I32 = mybir.dt.int32
U8 = mybir.dt.uint8
FP8X4 = mybir.dt.float8_e4m3fn_x4
FP4X4 = mybir.dt.float4_e2m1fn_x4
MULT = mybir.AluOpType.mult
ADD = mybir.AluOpType.add

P = 128
N = 512
TILES = S // P
CHUNKS = Q // N
STEPS = TILES * CHUNKS


def tile_reduced_heat_convection_g4_kernel(
    tc, a, c, ux_words, ux_scales, uy_words, uy_scales, tx_words, tx_scales, ty_words, ty_scales, w,
    out_0, out_1, out_2,
):
    nc = tc.nc
    with ExitStack() as ctx:
        keep = ctx.enter_context(tc.tile_pool(name="keep", bufs=1))
        work = ctx.enter_context(tc.tile_pool(name="work", bufs=3))
        psum = ctx.enter_context(tc.psum_pool(name="psum", bufs=1))
        ctx.enter_context(tc.manual_schedule())

        words_in = {"tx": tx_words, "ty": ty_words, "ux": ux_words, "uy": uy_words}
        scales_in = {"tx": tx_scales, "ty": ty_scales, "ux": ux_scales, "uy": uy_scales}
        passes = {"tx": RT // N, "ty": RT // N, "ux": RU // N, "uy": RU // N}

        ident = keep.tile([P, P], F32, name="ident")
        make_identity(nc, ident[:])

        planes = {}
        plane_tiles = {}

        def clear_plane(m, first, count):
            t = keep.tile([P, passes[m], N * count], U8, name="plane_%s_%d" % (m, first), align_bytes=64)
            nc.vector.memset(t[:].bitcast(I32), 0)
            plane_tiles[m, first] = t
            for j in range(count):
                for g in range(passes[m]):
                    planes[m, first + j, g] = t[:, g, N * j : N * (j + 1)]

        def load_scales(m, first, count, queue):
            rows = scales_in[m].bitcast(I32)[:, :, first * N // 4 : (first + count) * N // 4]
            for quad in range(4):
                queue.dma_start(
                    out=plane_tiles[m, first][32 * quad : 32 * quad + 4, :, :].bitcast(I32),
                    in_=rows[:, 4 * quad : 4 * quad + 4, :].rearrange("g r n -> r g n"),
                )

        weights = {}

        def load_words(m, first, count):
            t = keep.tile([P, passes[m], 2 * N * count], U8, name="words_%s_%d" % (m, first), align_bytes=64)
            src = words_in[m].bitcast(I32)[:, :, first * N // 2 : (first + count) * N // 2]
            nc.sync.dma_start(out=t[:].bitcast(I32), in_=src.rearrange("g p n -> p g n"))
            for j in range(count):
                for g in range(passes[m]):
                    weights[m, first + j, g] = t[:, g, 2 * N * j : 2 * N * (j + 1)]

        a_rows = {}
        c_rows = {}

        def load_a(i):
            a_rows[i] = keep.tile([P, RU], BF16, name="a_rows_%d" % i)
            nc.sync.dma_start(out=a_rows[i][:], in_=a[i * P : (i + 1) * P, :])

        def load_c(j):
            c_rows[j] = keep.tile([P, 2, RT], BF16, name="c_rows_%d" % j)
            nc.sync.dma_start(
                out=c_rows[j][:], in_=c[2 * j * P : 2 * (j + 1) * P, :].rearrange("(i p) k -> p i k", i=2)
            )

        w_cols = keep.tile([P, CHUNKS, 4], BF16, name="w_cols")
        w_psum = psum.tile([P, 2, 2, P], F32, name="w_bank")

        for m in ("tx", "ty", "ux", "uy"):
            clear_plane(m, 0, 1)
        load_c(0)
        load_a(0)
        load_scales("ty", 0, 1, nc.gpsimd)
        load_scales("tx", 0, 1, nc.sync)
        load_words("tx", 0, 1)
        load_words("ux", 0, 1)
        load_scales("ux", 0, 1, nc.sync)
        load_words("ty", 0, 1)
        load_words("uy", 0, 1)
        load_a(1)
        load_scales("uy", 0, 1, nc.sync)
        load_c(1)
        load_a(2)
        nc.sync.dma_start(out=w_cols[:], in_=w.rearrange("(g p j) -> p g j", g=CHUNKS, j=4))
        load_c(2)
        for i in range(3, TILES):
            load_a(i)
            if i == 4:
                load_c(3)

        out_words = out_1.rearrange("g p m t -> g p (m t)").bitcast(I32)
        out_scales = out_2.bitcast(I32)

        lhs = {}
        y_codes = {}
        y_scales = {}
        banks = {}
        grouped = {}
        d_sb = {}
        prods = {}
        sums = {}
        ys = {}
        y16 = {}
        w_bank = {}
        stored = {}
        sorted_rows = {}

        def turn(job):
            bank = psum.tile([P, 2, 2, P], F32, name="turn_bank", bufs=2)
            banks[job] = bank
            for h, (kind, i, k) in enumerate(job):
                for u in range(2):
                    if job in sorted_rows:
                        src = sorted_rows[job][:, h, u, :]
                    elif kind == "a":
                        src = a_rows[i][:].bitcast(F32)[:, 256 * k + u : 256 * (k + 1) : 2]
                    elif kind == "c":
                        src = c_rows[i // 2][:, i % 2, :].bitcast(F32)[:, u:256:2]
                    else:
                        src = y16[i][:].bitcast(F32)[:, P * u : P * (u + 1)]
                    nc.tensor.transpose(bank[:, h, u, :], src, ident[:])

        def presort(job):
            kind, i, k = job[0]
            rows = a_rows[i][:] if kind == "a" else c_rows[i // 2][:].rearrange("s h k -> s (h k)")
            sorted_rows[job] = work.tile([P, 2, 2, P], F32, name="sorted_rows", bufs=5)
            nc.vector.tensor_copy(
                out=sorted_rows[job][:], in_=rows.bitcast(F32).rearrange("s (h p u) -> s h u p", h=2, u=2)
            )

        def copy_out(job):
            t = work.tile([P, 2, N], BF16, name="grouped", bufs=4, align_bytes=64)
            grouped[job] = t[:, : len(job), :].rearrange("p h x -> p (h x)")
            nc.scalar.copy(
                out=grouped[job].bitcast(F32).rearrange("p (h s u) -> p h s u", s=P, u=2),
                in_=banks[job][:, : len(job), :, :].rearrange("p h u s -> p h s u"),
            )

        def quantize(job):
            width = P * len(job)
            if job[0][0] == "y":
                g, i = divmod(job[0][1], TILES)
                if i == 0:
                    y_codes[g] = keep.tile([P, S], U32, name="y_codes_%d" % g, align_bytes=64)
                    y_scales[g] = keep.tile([P, S], U8, name="y_scales_%d" % g, align_bytes=64)
                cols = slice(P * i, P * i + width)
                nc.vector.quantize_mx(
                    out=y_codes[g][:, cols].bitcast(FP8X4), scales=y_scales[g][:, cols], in_=grouped[job]
                )
                done = P * i + width
                if done % (S // 2) == 0 or job[0][1] >= STEPS - 4:
                    part = slice(stored.get(g, 0), done)
                    stored[g] = done
                    nc.sync.dma_start(out=out_words[g, :, part], in_=y_codes[g][:, part].bitcast(I32))
                if done == S:
                    for quad in range(4):
                        (nc.scalar if g == CHUNKS - 1 and quad % 2 else nc.sync).dma_start(
                            out=out_scales[g, 4 * quad : 4 * quad + 4, :],
                            in_=y_scales[g][32 * quad : 32 * quad + 4, :].bitcast(I32),
                        )
                return
            codes = keep.tile([P, width], U32, name="codes_%s_%d" % job[0][:2], align_bytes=64)
            scales = keep.tile([P, width], U8, name="scales_%s_%d" % job[0][:2], align_bytes=64)
            nc.vector.quantize_mx(out=codes[:].bitcast(FP8X4), scales=scales[:], in_=grouped[job])
            for h, key in enumerate(job):
                cols = slice(P * h, P * (h + 1))
                lhs[key] = (codes[:, cols], scales[:, cols])

        def product(m, n, bank):
            g, i = divmod(n, TILES)
            side = "a" if m[0] == "u" else "c"
            for k in range(passes[m]):
                codes, scales = lhs[side, i, k]
                nc.tensor.matmul_mx(
                    out=bank[:],
                    lhsT=codes.bitcast(FP8X4),
                    lhsT_scale=scales,
                    rhs=weights[m, g, k].bitcast(FP4X4),
                    rhs_scale=planes[m, g, k],
                    start=(k == 0),
                    stop=(k == passes[m] - 1),
                )

        def gradient(m, n):
            bank = psum.tile([P, N], F32, name="d_bank", bufs=2)
            product(m, n, bank)
            d_sb[m, n] = work.tile([P, N], F32, name="d_" + m)
            nc.scalar.copy(out=d_sb[m, n][:], in_=bank[:])

        def velocity(m, n):
            bank = psum.tile([P, N], F32, name="v_bank", bufs=3)
            product(m, n, bank)
            return bank

        def multiply(m, n, bank):
            prods[m, n] = work.tile([P, N], F32, name="prod_" + m)
            nc.vector.tensor_tensor(out=prods[m, n][:], in0=bank[:], in1=d_sb["t" + m[1], n][:], op=MULT)

        def add(n):
            sums[n] = work.tile([P, N], F32, name="sum")
            eng = nc.vector if n == STEPS - 1 else nc.gpsimd
            eng.tensor_tensor(out=sums[n][:], in0=prods["ux", n][:], in1=prods["uy", n][:], op=ADD)

        def weigh(n):
            g, i = divmod(n, TILES)
            ys[n] = work.tile([P, N], F32, name="y", bufs=6)
            nc.vector.tensor_tensor(
                out=ys[n][:].rearrange("s (p u e) -> s p u e", u=2, e=2),
                in0=sums[n][:].rearrange("s (p u e) -> s p u e", u=2, e=2),
                in1=w_bank[g].rearrange("s u p e -> s p u e"),
                op=MULT,
            )
            nc.sync.dma_start(out=out_0[i * P : (i + 1) * P, g * N : (g + 1) * N], in_=ys[n][:])

        def round_y(n):
            y16[n] = work.tile([P, N], BF16, name="y16", bufs=8)
            dst = y16[n][:].rearrange("s (u p e) -> s u p e", u=2, e=2)
            src = ys[n][:].rearrange("s (p u e) -> s u p e", u=2, e=2)
            if False:
                nc.gpsimd.tensor_scalar(out=dst, in0=src, scalar1=1.0, scalar2=1.0, op0=MULT, op1=MULT)
            else:
                nc.scalar.copy(out=dst, in_=src)

        def weigh_round(n):
            y16[n] = work.tile([P, N], BF16, name="y16", bufs=8)
            nc.vector.tensor_tensor(
                out=y16[n][:].rearrange("s (u p e) -> s u p e", u=2, e=2),
                in0=sums[n][:].rearrange("s (p u e) -> s u p e", u=2, e=2),
                in1=w_bank[n // TILES],
                op=MULT,
            )

        def spread_w(g):
            for u in range(2):
                col = w_cols[:, g, :].bitcast(F32)[:, u : u + 1]
                nc.tensor.transpose(w_psum[:, g % 2, u, :], col.to_broadcast([P, P]), ident[:])
            w_bank[g] = w_psum[:, g % 2, :, :].bitcast(BF16).rearrange("s u (p e) -> s u p e", e=2)

        def a_job(i):
            return (("a", i, 0), ("a", i, 1))

        def c_job(j):
            return (("c", 2 * j, 0), ("c", 2 * j + 1, 0))

        def y_job(m):
            return (("y", 2 * m, 0), ("y", 2 * m + 1, 0))

        runs = {-1: [a_job(1), c_job(1)], 0: [a_job(2), c_job(2)], 1: [a_job(3), a_job(4)], 2: [c_job(3), a_job(5)], 3: [a_job(6), a_job(7)]}
        for n in range(7, STEPS, 4):
            runs[n] = [y_job((n - 7) // 2), y_job((n - 5) // 2)]
        turn(c_job(0))
        turn(a_job(0))
        copy_out(c_job(0))
        quantize(c_job(0))
        copy_out(a_job(0))
        gradient("tx", 0)
        quantize(a_job(0))
        for m in ("tx", "ty", "ux", "uy"):
            clear_plane(m, 1, CHUNKS - 1)
            load_scales(m, 1, CHUNKS - 1, nc.sync)
        for m in ("tx", "ty", "ux", "uy"):
            load_words(m, 1, CHUNKS - 1)
        gradient("tx", 1)
        multiply("ux", 0, velocity("ux", 0))
        gradient("ty", 0)
        turn(a_job(1))
        turn(c_job(1))
        late = []
        for n in range(0, STEPS):
            turned = runs.get(n - 1, [])
            now = late + [j for j in turned[:1]] + [j for j in turned[1:] if j[0][0] != "y"]
            late = [j for j in turned[1:] if j[0][0] == "y"]
            ahead = n + 1 < STEPS
            if 0 <= n - 2:
                weigh(n - 2)
            for job in now[:1]:
                copy_out(job)
            if ahead and n > 0:
                gradient("tx", n + 1)
            for job in now[1:]:
                copy_out(job)
            if n > 0:
                multiply("ux", n, velocity("ux", n))
            if ahead:
                gradient("ty", n + 1)
            for job in now[:1]:
                quantize(job)
            if 0 <= n - 2:
                round_y(n - 2)
            for job in now[1:]:
                quantize(job)
            for job in runs.get(n + 1, []):
                if job[0][0] != "y" and n >= 1:
                    presort(job)
            multiply("uy", n, velocity("uy", n))
            if ahead:
                add(n)
            for job in runs.get(n, []):
                turn(job)
            if n == 1:
                spread_w(0)
                spread_w(1)
            if n == 11:
                spread_w(2)
        weigh(22)
        copy_out(y_job(8))
        turn(y_job(10))
        copy_out(y_job(9))
        round_y(22)
        add(23)
        weigh_round(23)
        weigh(23)
        turn(y_job(11))
        copy_out(y_job(10))
        quantize(y_job(8))
        quantize(y_job(9))
        quantize(y_job(10))
        copy_out(y_job(11))
        quantize(y_job(11))
